import numpy as np
import ml_dtypes


def mxq(x, axis, fmt="e4m3"):
    dtype, down = {"e4m3": (ml_dtypes.float8_e4m3fn, 7), "e5m2": (ml_dtypes.float8_e5m2, 14)}[fmt]
    v = np.moveaxis(np.asarray(x, np.float32).astype(ml_dtypes.bfloat16).astype(np.float64), axis, -1)
    blocks = v.reshape(v.shape[:-1] + (-1, 32))
    amax = np.abs(blocks).max(-1, keepdims=True)
    byte = np.maximum(np.where(amax > 0, np.frexp(amax)[1] - 1 + 127, 0) - down, 1)
    scale = np.exp2(byte - 127.0)
    codes = (blocks / scale).astype(np.float32).astype(dtype).astype(np.float64)
    return np.moveaxis((codes * scale).reshape(v.shape), -1, axis)


WIDE = False


def mx_kscale(k):
    if not WIDE:
        return np.ones(k)
    levels = np.array([10, -10, 5, -5, 0])
    if k % 512:
        return np.exp2(np.random.permutation(np.resize(levels, k // 32))).repeat(32)
    a = np.empty((k // 512, 16))
    for p in range(k // 512):
        a[p, :8] = np.random.permutation(np.resize(levels, 8))
        for g in range(8):
            far = levels[np.abs(levels - a[p, g]) >= 10]
            a[p, g + 8] = far[np.random.randint(len(far))]
    return np.exp2(a.ravel()).repeat(32)


def f64(x):
    return np.asarray(x).astype(np.float64)


def striped(idx):
    return np.tile(idx.reshape(-1, 16).T, (8, 1)).astype(np.uint16)


def unstriped(offs):
    return offs[:16].T.reshape(-1).astype(np.int64)


def pack_weight(w):
    k, n = w.shape
    w = f64(np.asarray(w, np.float32).astype(ml_dtypes.bfloat16)).reshape(k // 32, 32, n)
    amax = np.abs(w).max(1)
    byte = np.clip(np.where(amax > 0, np.frexp(amax)[1] - 1 + 127 - 7, 1), 1, 254)
    scaled = (w * np.exp2(127.0 - byte)[:, None, :]).reshape(k, n).astype(np.float32)
    words = np.ascontiguousarray(scaled.reshape(k // 512, 128, 4, n).transpose(0, 1, 3, 2)).astype(ml_dtypes.float8_e4m3fn).view(np.uint8)
    return words, np.ascontiguousarray(byte.astype(np.uint8).reshape(k // 512, 16, n))


def unpack_weight(words, scales):
    g, p, n, _ = words.shape
    vals = np.ascontiguousarray(words).view(ml_dtypes.float8_e4m3fn).astype(np.float64) * np.repeat(np.exp2(scales.astype(np.float64) - 127.0), 8, axis=1)[..., None]
    return vals.transpose(0, 1, 3, 2).reshape(g * 512, n)


K, T, S, N, H = 512, 2048, 512, 256, 512


def setup_inputs():
    n = np.random.standard_normal
    s = mx_kscale(K)[:, None]
    u = mx_kscale(H)
    packed_xT = pack_weight(n((K, T)) * s)
    return {
        "x_words": packed_xT[0],
        "x_scales": packed_xT[1],
        "w1": (n((K, H)) / np.sqrt(K) / s).astype(np.float32),
        "w2": (n((K, H)) / np.sqrt(K) / s).astype(np.float32),
        "twr": (np.random.uniform(-1.0, 1.0, (H, S))).astype(np.float32),
        "twi": (np.random.uniform(-1.0, 1.0, (H, S))).astype(np.float32),
        "unit": (np.random.uniform(0.6, 1.4, (H, 1)) * u[:, None]).astype(np.float32),
        "w3": (n((H, N)) / np.sqrt(H) / u[:, None]).astype(np.float32),
        "offs": striped(np.random.permutation(T)[:S]),
        "b1": striped(np.random.permutation(S)),
        "b2": striped(np.random.permutation(S)),
    }


def reference(x_words, x_scales, w1, w2, twr, twi, unit, w3, offs, b1, b2):
    xq = unpack_weight(x_words, x_scales)[:, unstriped(offs)]
    re = mxq(f64(w1), 0, "e4m3").T @ xq
    pr = re[:, unstriped(b1)]
    im2 = mxq(f64(w2), 0, "e4m3").T @ xq
    pi1 = im2[:, unstriped(b1)]
    xr = re + f64(twr) * pr - (f64(twi) * pi1)
    xp = xr[:, unstriped(b2)]
    yr1 = xr - xp
    xi = im2 + f64(twr) * pi1 + f64(twi) * pr
    xq = xi[:, unstriped(b2)]
    yi1 = xi + xq
    hid = f64(unit) * (np.sqrt((yr1) ** 2 + (yi1) ** 2 + 0.1))
    return mxq(f64(w3), 0, "e4m3").T @ mxq(hid, 0, "e4m3")

@@ -1,0 +1,278 @@
+from contextlib import ExitStack
+
+import concourse.mybir as mybir
+from concourse.masks import make_identity
+
+K, T, S, N, H = 512, 2048, 512, 256, 512
+FLOPS = 2 * K * H * S * 2 + 2 * H * N * S
+
+F32 = mybir.dt.float32
+BF16 = mybir.dt.bfloat16
+I32 = mybir.dt.int32
+U32 = mybir.dt.uint32
+U16 = mybir.dt.uint16
+U8 = mybir.dt.uint8
+FP8X4 = mybir.dt.float8_e4m3fn_x4
+ACT = mybir.ActivationFunctionType
+ALU = mybir.AluOpType
+
+P = 128
+PACK = 4
+HALF = S // 2
+LIST_COLS = S // 16
+
+
+def tile_picked_ybutfly_mag_p_kernel(
+    tc, x_words, x_scales, w1, w2, twr, twi, unit, w3, offs, b1, b2, out
+):
+    nc = tc.nc
+    with ExitStack() as ctx:
+        keep = ctx.enter_context(tc.tile_pool(name="keep", bufs=1))
+        work = ctx.enter_context(tc.tile_pool(name="work", bufs=2))
+        mm_ps = ctx.enter_context(tc.psum_pool(name="mm_ps", bufs=2))
+        fwd_ps = ctx.enter_context(tc.psum_pool(name="fwd_ps", bufs=4))
+        back_ps = ctx.enter_context(tc.psum_pool(name="back_ps", bufs=2))
+
+        def held(shape, dtype, name):
+            return keep.tile(shape, dtype, name=name, align_bytes=64)
+
+        offs_sb = held([P, LIST_COLS], U16, "offs_sb")
+        b1_sb = held([P, LIST_COLS], U16, "b1_sb")
+        b2_sb = held([P, LIST_COLS], U16, "b2_sb")
+        scale_table = held([P, T], U8, "scale_table")
+        word_table = held([P, T], U32, "word_table")
+        w1_raw = held([P, PACK, H], F32, "w1_raw")
+        w2_raw = held([P, PACK, H], F32, "w2_raw")
+        w3_raw = held([P, PACK, N], F32, "w3_raw")
+        unit_sb = held([P, PACK], F32, "unit_sb")
+        twr_sb = [held([P, S], F32, "twr%d" % t) for t in range(PACK)]
+        twi_sb = [held([P, S], F32, "twi%d" % t) for t in range(PACK)]
+
+        nc.vector.memset(scale_table[:, : T // 2].bitcast(I32), 0)
+        nc.gpsimd.memset(scale_table[:, T // 2 :].bitcast(I32), 0)
+        nc.sync.dma_start(out=w1_raw[:], in_=w1.rearrange("(p j) c -> p j c", j=PACK))
+        nc.sync.dma_start(offs_sb[:], offs)
+        nc.sync.dma_start(b1_sb[:], b1)
+        for q in range(4):
+            nc.sync.dma_start(
+                out=scale_table[32 * q : 32 * q + 4, :].bitcast(I32),
+                in_=x_scales[0, 4 * q : 4 * q + 4, :].bitcast(I32),
+            )
+        nc.sync.dma_start(
+            out=word_table[:].bitcast(I32),
+            in_=x_words[0].rearrange("p n t -> p (n t)").bitcast(I32),
+        )
+        nc.sync.dma_start(out=w2_raw[:], in_=w2.rearrange("(p j) c -> p j c", j=PACK))
+        twr_rows = twr.rearrange("(p t) s -> p t s", t=PACK)
+        twi_rows = twi.rearrange("(p t) s -> p t s", t=PACK)
+        for t in range(PACK):
+            nc.sync.dma_start(out=twr_sb[t][:], in_=twr_rows[:, t, :])
+            nc.sync.dma_start(out=twi_sb[t][:], in_=twi_rows[:, t, :])
+            if t == 0:
+                nc.sync.dma_start(b2_sb[:], b2)
+        nc.sync.dma_start(out=unit_sb[:], in_=unit.rearrange("(p t) o -> p (t o)", t=PACK))
+        nc.sync.dma_start(out=w3_raw[:], in_=w3.rearrange("(p j) c -> p j c", j=PACK))
+
+        ident = held([P, P], F32, "ident")
+        make_identity(nc, ident[:])
+        one = held([P, 1], F32, "one")
+        eps = held([P, 1], F32, "eps")
+        nc.gpsimd.memset(one[:], 1.0)
+        nc.gpsimd.tensor_scalar(eps[:], one[:], 0.1, 0.0, ALU.mult, ALU.add)
+
+        def copy_on(engine, dst, src):
+            if engine == "V":
+                nc.vector.tensor_copy(out=dst, in_=src)
+            else:
+                nc.scalar.copy(out=dst, in_=src)
+
+        def quantise_pair(raw, pair, engine, name):
+            grouped = held([P, 2 * P * PACK], BF16, name + "_bf")
+            codes = held([P, 2 * P], U32, name + "_codes")
+            scales = held([P, 2 * P], U8, name + "_scales")
+            copy_on(
+                engine,
+                grouped[:].rearrange("p (t m j) -> p m j t", t=2, j=PACK),
+                raw[:].rearrange("p j (m t) -> p m j t", t=PACK)[:, :, :, 2 * pair : 2 * pair + 2],
+            )
+            nc.vector.quantize_mx(out=codes[:].bitcast(FP8X4), scales=scales[:], in_=grouped[:])
+            return codes, scales
+
+        w1_q = [quantise_pair(w1_raw, 0, "V", "w1a"), quantise_pair(w1_raw, 1, "S", "w1b")]
+
+        x_scale = held([P, S], U8, "x_scale")
+        x_code = held([P, S], U32, "x_code")
+        nc.vector.tensor_copy(out=x_scale[:], in_=scale_table[:].indirect(offs_sb[:]))
+        nc.vector.tensor_copy(out=x_code[:], in_=word_table[:].indirect(offs_sb[:]))
+
+        def product(w_q, t, name):
+            codes, scales = w_q[t // 2]
+            cols = slice((t % 2) * P, (t % 2 + 1) * P)
+            acc = mm_ps.tile([P, S], F32, tag="mm", name="acc_" + name)
+            nc.tensor.matmul_mx(
+                out=acc[:],
+                lhsT=codes[:, cols].bitcast(FP8X4),
+                lhsT_scale=scales[:, cols],
+                rhs=x_code[:].bitcast(FP8X4),
+                rhs_scale=x_scale[:],
+                start=True,
+                stop=True,
+            )
+            rows = held([P, S], F32, name)
+            nc.scalar.copy(out=rows[:], in_=acc[:])
+            return rows
+
+        def gather(engine, dst, window, places, scale=None):
+            picked = window[:].indirect(places)
+            if scale is not None:
+                nc.scalar.activation(out=dst, in_=picked, func=ACT.Copy, scale=scale)
+            elif engine == "V":
+                nc.vector.tensor_copy(out=dst, in_=picked)
+            else:
+                nc.scalar.activation(out=dst, in_=picked, func=ACT.Copy)
+
+        PR, PI, XQ, EO = "VSVS", "SSSS", "SVVV", "VSVS"
+        PARTS = [2,2,2,4]
+        LAST = PARTS[3]
+        LW = S // LAST
+        re, im, pr, pi, xr, xi, xp, xq, mag = {}, {}, {}, {}, {}, {}, {}, {}, {}
+        pairs = [held([P, 2, LW, 2], BF16, "pairs%d" % h) for h in range(LAST)]
+
+        def partners(t):
+            pr[t] = held([P, S], F32, "pr%d" % t)
+            pi[t] = held([P, S], F32, "pi%d" % t)
+            for dst, window, engine in ((pr[t], re[t], PR[t]), (pi[t], im[t], PI[t])):
+                for h in range(2):
+                    gather(engine, dst[:, h * HALF : (h + 1) * HALF], window, b1_sb[:, h * 16 : (h + 1) * 16])
+
+        def first_stage(t):
+            a = work.tile([P, S], F32, tag="a", name="a")
+            e = work.tile([P, S], F32, tag="e", name="e")
+            b = work.tile([P, S], F32, tag="b", name="b")
+            c = work.tile([P, S], F32, tag="c", name="c")
+            u = work.tile([P, S], F32, tag="u", name="u")
+            v = work.tile([P, S], F32, tag="v", name="v")
+            xr[t] = held([P, S], F32, "xr%d" % t)
+            xi[t] = held([P, S], F32, "xi%d" % t)
+            nc.vector.tensor_tensor(a[:], pr[t][:], twr_sb[t][:], ALU.mult)
+            nc.vector.tensor_tensor(e[:], pr[t][:], twi_sb[t][:], ALU.mult)
+            nc.vector.tensor_tensor(u[:], re[t][:], a[:], ALU.add)
+            nc.vector.tensor_tensor(v[:], im[t][:], e[:], ALU.add)
+            nc.vector.tensor_tensor(b[:], pi[t][:], twi_sb[t][:], ALU.mult)
+            nc.vector.tensor_tensor(c[:], pi[t][:], twr_sb[t][:], ALU.mult)
+            nc.vector.tensor_tensor(xr[t][:], u[:], b[:], ALU.subtract)
+            nc.vector.tensor_tensor(xi[t][:], v[:], c[:], ALU.add)
+
+        def turned_sum(acc, terms):
+            for n, (blk, source) in enumerate(terms):
+                nc.tensor.matmul(
+                    acc[:, blk * P : (blk + 1) * P], lhsT=source, rhs=ident[:], is_transpose=True,
+                    start=(n == 0), stop=(n == len(terms) - 1),
+                )
+
+        def second_partners(t):
+            width = S // PARTS[t]
+            xp[t] = held([P, S], F32, "xp%d" % t)
+            xq[t] = held([P, S], F32, "xq%d" % t)
+            for h in range(PARTS[t]):
+                cols = slice(h * width, (h + 1) * width)
+                places = b2_sb[:, h * width // 16 : (h + 1) * width // 16]
+                gather("S", xp[t][:, cols], xr[t], places, scale=-1.0)
+                gather(XQ[t], xq[t][:, cols], xi[t], places)
+
+        def second_stage(t):
+            width = S // PARTS[t]
+            nblk = width // P
+            squares = []
+            for h in range(PARTS[t]):
+                y = fwd_ps.tile([P, 2 * width], F32, tag="fwd", name="y")
+                terms = []
+                for first, source in ((0, xr[t]), (nblk, xi[t]), (0, xp[t]), (nblk, xq[t])):
+                    for k in range(nblk):
+                        terms.append((first + k, source[:, h * width + k * P : h * width + (k + 1) * P]))
+                turned_sum(y, terms)
+                sq = held([P, 2 * width], F32, "sq%d_%d" % (t, h))
+                nc.scalar.activation(out=sq[:], in_=y[:], func=ACT.Square)
+                squares.append(sq)
+            mag[t] = held([P, S], F32, "mag%d" % t)
+            for h in range(PARTS[t]):
+                power = back_ps.tile([P, width], F32, tag="back", name="power")
+                turned_sum(power, [(k % nblk, squares[h][:, k * P : (k + 1) * P]) for k in range(2 * nblk)])
+                nc.scalar.activation(out=mag[t][:, h * width : (h + 1) * width], in_=power[:], func=ACT.Sqrt, bias=eps[:])
+
+        def scale_rows(t, h):
+            nc.vector.tensor_scalar(
+                pairs[h][:, t // 2, :, t % 2], mag[t][:, h * LW : (h + 1) * LW], unit_sb[:, t : t + 1], None, ALU.mult,
+            )
+
+        w3_bf = held([P, N * PACK], BF16, "w3_bf")
+        w3_codes = held([P, N], U32, "w3_codes")
+        w3_scales = held([P, N], U8, "w3_scales")
+
+        def third_weight():
+            nc.vector.tensor_copy(
+                out=w3_bf[:].rearrange("p (n j) -> p n j", j=PACK), in_=w3_raw[:].rearrange("p j n -> p n j")
+            )
+            nc.vector.quantize_mx(out=w3_codes[:].bitcast(FP8X4), scales=w3_scales[:], in_=w3_bf[:])
+
+        re[0] = product(w1_q, 0, "re0")
+        w2_q = [quantise_pair(w2_raw, 0, "V", "w2a")]
+        im[0] = product(w2_q, 0, "im0")
+        re[1] = product(w1_q, 1, "re1")
+        partners(0)
+        im[1] = product(w2_q, 1, "im1")
+        partners(1)
+        first_stage(0)
+        w2_q.append(quantise_pair(w2_raw, 1, "S", "w2b"))
+        re[2] = product(w1_q, 2, "re2")
+        im[2] = product(w2_q, 2, "im2")
+        partners(2)
+        first_stage(1)
+        re[3] = product(w1_q, 3, "re3")
+        im[3] = product(w2_q, 3, "im3")
+        second_partners(0)
+        partners(3)
+        second_stage(0)
+        first_stage(2)
+        second_partners(1)
+        second_stage(1)
+        first_stage(3)
+        second_partners(2)
+        second_partners(3)
+        second_stage(2)
+        third_weight()
+        for h in range(LAST):
+            scale_rows(0, h)
+        for h in range(LAST):
+            scale_rows(1, h)
+        second_stage(3)
+        for h in range(LAST):
+            scale_rows(2, h)
+
+        for h in range(LAST):
+            scale_rows(3, h)
+            hid = held([P, LW * PACK], BF16, "hid%d" % h)
+            nc.vector.tensor_copy(
+                out=hid[:].bitcast(I32).rearrange("p (n u) -> p n u", u=2),
+                in_=pairs[h][:].rearrange("p u n e -> p (u n e)").bitcast(I32).rearrange("p (u n) -> p n u", u=2),
+            )
+            hid_codes = held([P, LW], U32, "hid_codes%d" % h)
+            hid_scales = held([P, LW], U8, "hid_scales%d" % h)
+            nc.vector.quantize_mx(out=hid_codes[:].bitcast(FP8X4), scales=hid_scales[:], in_=hid[:])
+            acc = mm_ps.tile([P, 2 * LW], F32, tag="mm", name="acc_out")
+            for m in range(2):
+                cols = slice(m * P, (m + 1) * P)
+                nc.tensor.matmul_mx(
+                    out=acc[:, m * LW : (m + 1) * LW],
+                    lhsT=w3_codes[:, cols].bitcast(FP8X4),
+                    lhsT_scale=w3_scales[:, cols],
+                    rhs=hid_codes[:].bitcast(FP8X4),
+                    rhs_scale=hid_scales[:],
+                    start=True,
+                    stop=True,
+                )
+            result = held([P, 2, LW], F32, "result%d" % h)
+            copy_on(EO[h], result[:].rearrange("p m n -> p (m n)"), acc[:])
+            nc.sync.dma_start(
+                out=out.rearrange("(m p) s -> p m s", p=P)[:, :, h * LW : (h + 1) * LW], in_=result[:]
+            )

@@ -18,8 +18,11 @@ ALU = mybir.AluOpType
 
 P = 128
 PACK = 4
-HALF = S // 2
 LIST_COLS = S // 16
+PARTS = [2,2,2,4]
+LAST = PACK - 1
+PIECES = PARTS[LAST]
+PIECE = S // PIECES
 
 
 def tile_picked_ybutfly_mag_p_kernel(
@@ -29,9 +32,8 @@ def tile_picked_ybutfly_mag_p_kernel(
     with ExitStack() as ctx:
         keep = ctx.enter_context(tc.tile_pool(name="keep", bufs=1))
         work = ctx.enter_context(tc.tile_pool(name="work", bufs=2))
-        mm_ps = ctx.enter_context(tc.psum_pool(name="mm_ps", bufs=2))
-        fwd_ps = ctx.enter_context(tc.psum_pool(name="fwd_ps", bufs=4))
-        back_ps = ctx.enter_context(tc.psum_pool(name="back_ps", bufs=2))
+        sums_ps = ctx.enter_context(tc.psum_pool(name="sums_ps", bufs=5))
+        power_ps = ctx.enter_context(tc.psum_pool(name="power_ps", bufs=3))
 
         def held(shape, dtype, name):
             return keep.tile(shape, dtype, name=name, align_bytes=64)
@@ -45,8 +47,8 @@ def tile_picked_ybutfly_mag_p_kernel(
         w2_raw = held([P, PACK, H], F32, "w2_raw")
         w3_raw = held([P, PACK, N], F32, "w3_raw")
         unit_sb = held([P, PACK], F32, "unit_sb")
-        twr_sb = [held([P, S], F32, "twr%d" % t) for t in range(PACK)]
-        twi_sb = [held([P, S], F32, "twi%d" % t) for t in range(PACK)]
+        rows = [held([P, 4 * S], F32, "rows%d" % t) for t in range(PACK)]
+        RE, TWR, IM, TWI = [slice(n * S, (n + 1) * S) for n in range(4)]
 
         nc.vector.memset(scale_table[:, : T // 2].bitcast(I32), 0)
         nc.gpsimd.memset(scale_table[:, T // 2 :].bitcast(I32), 0)
@@ -66,8 +68,8 @@ def tile_picked_ybutfly_mag_p_kernel(
         twr_rows = twr.rearrange("(p t) s -> p t s", t=PACK)
         twi_rows = twi.rearrange("(p t) s -> p t s", t=PACK)
         for t in range(PACK):
-            nc.sync.dma_start(out=twr_sb[t][:], in_=twr_rows[:, t, :])
-            nc.sync.dma_start(out=twi_sb[t][:], in_=twi_rows[:, t, :])
+            nc.sync.dma_start(out=rows[t][:, TWR], in_=twr_rows[:, t, :])
+            nc.sync.dma_start(out=rows[t][:, TWI], in_=twi_rows[:, t, :])
             if t == 0:
                 nc.sync.dma_start(b2_sb[:], b2)
         nc.sync.dma_start(out=unit_sb[:], in_=unit.rearrange("(p t) o -> p (t o)", t=PACK))
@@ -105,10 +107,10 @@ def tile_picked_ybutfly_mag_p_kernel(
         nc.vector.tensor_copy(out=x_scale[:], in_=scale_table[:].indirect(offs_sb[:]))
         nc.vector.tensor_copy(out=x_code[:], in_=word_table[:].indirect(offs_sb[:]))
 
-        def product(w_q, t, name):
+        def product(w_q, t, part):
             codes, scales = w_q[t // 2]
             cols = slice((t % 2) * P, (t % 2 + 1) * P)
-            acc = mm_ps.tile([P, S], F32, tag="mm", name="acc_" + name)
+            acc = sums_ps.tile([P, S], F32, tag="sums", name="acc")
             nc.tensor.matmul_mx(
                 out=acc[:],
                 lhsT=codes[:, cols].bitcast(FP8X4),
@@ -118,12 +120,10 @@ def tile_picked_ybutfly_mag_p_kernel(
                 start=True,
                 stop=True,
             )
-            rows = held([P, S], F32, name)
-            nc.scalar.copy(out=rows[:], in_=acc[:])
-            return rows
+            nc.scalar.copy(out=rows[t][:, part], in_=acc[:])
 
         def gather(engine, dst, window, places, scale=None):
-            picked = window[:].indirect(places)
+            picked = window.indirect(places)
             if scale is not None:
                 nc.scalar.activation(out=dst, in_=picked, func=ACT.Copy, scale=scale)
             elif engine == "V":
@@ -131,37 +131,35 @@ def tile_picked_ybutfly_mag_p_kernel(
             else:
                 nc.scalar.activation(out=dst, in_=picked, func=ACT.Copy)
 
-        PR, PI, XQ, EO = "VSVS", "SSSS", "SVVV", "VSVS"
-        PARTS = [2,2,2,4]
-        LAST = PARTS[3]
-        LW = S // LAST
-        re, im, pr, pi, xr, xi, xp, xq, mag = {}, {}, {}, {}, {}, {}, {}, {}, {}
-        pairs = [held([P, 2, LW, 2], BF16, "pairs%d" % h) for h in range(LAST)]
+        PR, PI, XQ, EO = "SVVS", "SSSS", "VSSV", "SSSS"
+        pr = [held([P, S], F32, "pr%d" % t) for t in range(PACK)]
+        pi = [held([P, S], F32, "pi%d" % t) for t in range(PACK)]
+        xr = [held([P, S], F32, "xr%d" % t) for t in range(PACK)]
+        xi = [held([P, S], F32, "xi%d" % t) for t in range(PACK)]
+        xp = [held([P, S], F32, "xp%d" % t) for t in range(PACK)]
+        xq = [held([P, S], F32, "xq%d" % t) for t in range(PACK)]
+        mag = held([P, PACK, S], F32, "mag")
+        squares = {}
+        hid = [held([P, PIECE * PACK], BF16, "hid%d" % h) for h in range(PIECES)]
 
-        def partners(t):
-            pr[t] = held([P, S], F32, "pr%d" % t)
-            pi[t] = held([P, S], F32, "pi%d" % t)
-            for dst, window, engine in ((pr[t], re[t], PR[t]), (pi[t], im[t], PI[t])):
-                for h in range(2):
-                    gather(engine, dst[:, h * HALF : (h + 1) * HALF], window, b1_sb[:, h * 16 : (h + 1) * 16])
+        def real_partner(t):
+            gather(PR[t], pr[t][:], rows[t][:, 0 : 2 * S], b1_sb[:])
+
+        def imag_partner(t):
+            gather(PI[t], pi[t][:], rows[t][:, 2 * S : 4 * S], b1_sb[:])
 
         def first_stage(t):
-            a = work.tile([P, S], F32, tag="a", name="a")
-            e = work.tile([P, S], F32, tag="e", name="e")
-            b = work.tile([P, S], F32, tag="b", name="b")
-            c = work.tile([P, S], F32, tag="c", name="c")
+            twiddles = rows[t][:].rearrange("p (a b s) -> p a b s", a=2, b=2)[:, :, 1, :]
+            by_pr = work.tile([P, 2, S], F32, tag="by_pr", name="by_pr")
+            by_pi = work.tile([P, 2, S], F32, tag="by_pi", name="by_pi")
             u = work.tile([P, S], F32, tag="u", name="u")
             v = work.tile([P, S], F32, tag="v", name="v")
-            xr[t] = held([P, S], F32, "xr%d" % t)
-            xi[t] = held([P, S], F32, "xi%d" % t)
-            nc.vector.tensor_tensor(a[:], pr[t][:], twr_sb[t][:], ALU.mult)
-            nc.vector.tensor_tensor(e[:], pr[t][:], twi_sb[t][:], ALU.mult)
-            nc.vector.tensor_tensor(u[:], re[t][:], a[:], ALU.add)
-            nc.vector.tensor_tensor(v[:], im[t][:], e[:], ALU.add)
-            nc.vector.tensor_tensor(b[:], pi[t][:], twi_sb[t][:], ALU.mult)
-            nc.vector.tensor_tensor(c[:], pi[t][:], twr_sb[t][:], ALU.mult)
-            nc.vector.tensor_tensor(xr[t][:], u[:], b[:], ALU.subtract)
-            nc.vector.tensor_tensor(xi[t][:], v[:], c[:], ALU.add)
+            nc.vector.tensor_tensor(by_pr[:], twiddles, pr[t][:].unsqueeze(1).to_broadcast([P, 2, S]), ALU.mult)
+            nc.vector.tensor_tensor(by_pi[:], twiddles, pi[t][:].unsqueeze(1).to_broadcast([P, 2, S]), ALU.mult)
+            nc.vector.tensor_tensor(u[:], rows[t][:, RE], by_pr[:, 0, :], ALU.add)
+            nc.vector.tensor_tensor(v[:], rows[t][:, IM], by_pr[:, 1, :], ALU.add)
+            nc.vector.tensor_tensor(xr[t][:], u[:], by_pi[:, 1, :], ALU.subtract)
+            nc.vector.tensor_tensor(xi[t][:], v[:], by_pi[:, 0, :], ALU.add)
 
         def turned_sum(acc, terms):
             for n, (blk, source) in enumerate(terms):
@@ -172,98 +170,102 @@ def tile_picked_ybutfly_mag_p_kernel(
 
         def second_partners(t):
             width = S // PARTS[t]
-            xp[t] = held([P, S], F32, "xp%d" % t)
-            xq[t] = held([P, S], F32, "xq%d" % t)
             for h in range(PARTS[t]):
                 cols = slice(h * width, (h + 1) * width)
                 places = b2_sb[:, h * width // 16 : (h + 1) * width // 16]
-                gather("S", xp[t][:, cols], xr[t], places, scale=-1.0)
-                gather(XQ[t], xq[t][:, cols], xi[t], places)
+                gather("S", xp[t][:, cols], xr[t][:], places, scale=-1.0)
+                gather(XQ[t], xq[t][:, cols], xi[t][:], places)
 
-        def second_stage(t):
+        def square_parts(t):
             width = S // PARTS[t]
             nblk = width // P
-            squares = []
             for h in range(PARTS[t]):
-                y = fwd_ps.tile([P, 2 * width], F32, tag="fwd", name="y")
+                y = sums_ps.tile([P, 2 * width], F32, tag="sums", name="y")
+                sources = [(0, xr[t]), (nblk, xi[t]), (0, xp[t]), (nblk, xq[t])]
+                if t == LAST:
+                    sources = [(0, xr[t]), (nblk, xi[t]), (nblk, xq[t]), (0, xp[t])]
                 terms = []
-                for first, source in ((0, xr[t]), (nblk, xi[t]), (0, xp[t]), (nblk, xq[t])):
+                for first, source in sources:
                     for k in range(nblk):
                         terms.append((first + k, source[:, h * width + k * P : h * width + (k + 1) * P]))
                 turned_sum(y, terms)
-                sq = held([P, 2 * width], F32, "sq%d_%d" % (t, h))
-                nc.scalar.activation(out=sq[:], in_=y[:], func=ACT.Square)
-                squares.append(sq)
-            mag[t] = held([P, S], F32, "mag%d" % t)
-            for h in range(PARTS[t]):
-                power = back_ps.tile([P, width], F32, tag="back", name="power")
-                turned_sum(power, [(k % nblk, squares[h][:, k * P : (k + 1) * P]) for k in range(2 * nblk)])
-                nc.scalar.activation(out=mag[t][:, h * width : (h + 1) * width], in_=power[:], func=ACT.Sqrt, bias=eps[:])
+                squares[t, h] = held([P, 2 * width], F32, "sq%d_%d" % (t, h))
+                nc.scalar.activation(out=squares[t, h][:], in_=y[:], func=ACT.Square)
 
-        def scale_rows(t, h):
-            nc.vector.tensor_scalar(
-                pairs[h][:, t // 2, :, t % 2], mag[t][:, h * LW : (h + 1) * LW], unit_sb[:, t : t + 1], None, ALU.mult,
-            )
+        def magnitudes(t):
+            width = S // PARTS[t]
+            nblk = width // P
+            for h in range(PARTS[t]):
+                power = power_ps.tile([P, width], F32, tag="power", name="power")
+                turned_sum(power, [(k % nblk, squares[t, h][:, k * P : (k + 1) * P]) for k in range(2 * nblk)])
+                nc.scalar.activation(out=mag[:, t, h * width : (h + 1) * width], in_=power[:], func=ACT.Sqrt, bias=eps[:])
+
+        product(w1_q, 0, RE)
+        w2_q = [quantise_pair(w2_raw, 0, "V", "w2a")]
+        product(w2_q, 0, IM)
+        real_partner(0)
+        imag_partner(0)
+        w2_q.append(quantise_pair(w2_raw, 1, "V", "w2b"))
+        product(w1_q, 1, RE)
+        product(w2_q, 1, IM)
+        real_partner(1)
+        imag_partner(1)
+        first_stage(0)
+        product(w1_q, 2, RE)
+        product(w2_q, 2, IM)
+        real_partner(2)
+        imag_partner(2)
+        first_stage(1)
+        second_partners(0)
+        product(w1_q, 3, RE)
+        product(w2_q, 3, IM)
+        square_parts(0)
+        real_partner(3)
+        imag_partner(3)
+        magnitudes(0)
+        first_stage(2)
+        second_partners(1)
+        square_parts(1)
+        magnitudes(1)
+        first_stage(3)
+        second_partners(2)
+        second_partners(3)
+        square_parts(2)
+        magnitudes(2)
+        square_parts(3)
+        magnitudes(3)
 
         w3_bf = held([P, N * PACK], BF16, "w3_bf")
         w3_codes = held([P, N], U32, "w3_codes")
         w3_scales = held([P, N], U8, "w3_scales")
+        nc.vector.tensor_copy(
+            out=w3_bf[:].rearrange("p (c i j) -> p c j i", i=4, j=PACK),
+            in_=w3_raw[:].rearrange("p j (c i) -> p c j i", i=4),
+        )
+        nc.vector.quantize_mx(out=w3_codes[:].bitcast(FP8X4), scales=w3_scales[:], in_=w3_bf[:])
 
-        def third_weight():
-            nc.vector.tensor_copy(
-                out=w3_bf[:].rearrange("p (n j) -> p n j", j=PACK), in_=w3_raw[:].rearrange("p j n -> p n j")
+        for h in range(PIECES):
+            nc.vector.tensor_tensor(
+                hid[h][:].rearrange("p (c i t) -> p c t i", i=4, t=PACK)[:, :, 0:LAST, :],
+                mag[:, 0:LAST, h * PIECE : (h + 1) * PIECE].rearrange("p t (c i) -> p c t i", i=4),
+                unit_sb[:, 0:LAST].unsqueeze(1).unsqueeze(3).to_broadcast([P, PIECE // 4, LAST, 4]),
+                ALU.mult,
             )
-            nc.vector.quantize_mx(out=w3_codes[:].bitcast(FP8X4), scales=w3_scales[:], in_=w3_bf[:])
 
-        re[0] = product(w1_q, 0, "re0")
-        w2_q = [quantise_pair(w2_raw, 0, "V", "w2a")]
-        im[0] = product(w2_q, 0, "im0")
-        re[1] = product(w1_q, 1, "re1")
-        partners(0)
-        im[1] = product(w2_q, 1, "im1")
-        partners(1)
-        first_stage(0)
-        w2_q.append(quantise_pair(w2_raw, 1, "S", "w2b"))
-        re[2] = product(w1_q, 2, "re2")
-        im[2] = product(w2_q, 2, "im2")
-        partners(2)
-        first_stage(1)
-        re[3] = product(w1_q, 3, "re3")
-        im[3] = product(w2_q, 3, "im3")
-        second_partners(0)
-        partners(3)
-        second_stage(0)
-        first_stage(2)
-        second_partners(1)
-        second_stage(1)
-        first_stage(3)
-        second_partners(2)
-        second_partners(3)
-        second_stage(2)
-        third_weight()
-        for h in range(LAST):
-            scale_rows(0, h)
-        for h in range(LAST):
-            scale_rows(1, h)
-        second_stage(3)
-        for h in range(LAST):
-            scale_rows(2, h)
-
-        for h in range(LAST):
-            scale_rows(3, h)
-            hid = held([P, LW * PACK], BF16, "hid%d" % h)
-            nc.vector.tensor_copy(
-                out=hid[:].bitcast(I32).rearrange("p (n u) -> p n u", u=2),
-                in_=pairs[h][:].rearrange("p u n e -> p (u n e)").bitcast(I32).rearrange("p (u n) -> p n u", u=2),
+        for h in range(PIECES):
+            nc.vector.tensor_scalar(
+                hid[h][:].rearrange("p (n t) -> p n t", t=PACK)[:, :, LAST],
+                mag[:, LAST, h * PIECE : (h + 1) * PIECE],
+                unit_sb[:, LAST : LAST + 1], None, ALU.mult,
             )
-            hid_codes = held([P, LW], U32, "hid_codes%d" % h)
-            hid_scales = held([P, LW], U8, "hid_scales%d" % h)
-            nc.vector.quantize_mx(out=hid_codes[:].bitcast(FP8X4), scales=hid_scales[:], in_=hid[:])
-            acc = mm_ps.tile([P, 2 * LW], F32, tag="mm", name="acc_out")
+            hid_codes = held([P, PIECE], U32, "hid_codes%d" % h)
+            hid_scales = held([P, PIECE], U8, "hid_scales%d" % h)
+            nc.vector.quantize_mx(out=hid_codes[:].bitcast(FP8X4), scales=hid_scales[:], in_=hid[h][:])
+            acc = sums_ps.tile([P, 2 * PIECE], F32, tag="sums", name="acc_out")
             for m in range(2):
                 cols = slice(m * P, (m + 1) * P)
                 nc.tensor.matmul_mx(
-                    out=acc[:, m * LW : (m + 1) * LW],
+                    out=acc[:, m * PIECE : (m + 1) * PIECE],
                     lhsT=w3_codes[:, cols].bitcast(FP8X4),
                     lhsT_scale=w3_scales[:, cols],
                     rhs=hid_codes[:].bitcast(FP8X4),
@@ -271,8 +273,8 @@ def tile_picked_ybutfly_mag_p_kernel(
                     start=True,
                     stop=True,
                 )
-            result = held([P, 2, LW], F32, "result%d" % h)
+            result = held([P, 2, PIECE], F32, "result%d" % h)
             copy_on(EO[h], result[:].rearrange("p m n -> p (m n)"), acc[:])
             nc.sync.dma_start(
-                out=out.rearrange("(m p) s -> p m s", p=P)[:, :, h * LW : (h + 1) * LW], in_=result[:]
+                out=out.rearrange("(m p) s -> p m s", p=P)[:, :, h * PIECE : (h + 1) * PIECE], in_=result[:]
             )

@@ -81,6 +81,8 @@ def tile_picked_ybutfly_mag_p_kernel(
         eps = held([P, 1], F32, "eps")
         nc.gpsimd.memset(one[:], 1.0)
         nc.gpsimd.tensor_scalar(eps[:], one[:], 0.1, 0.0, ALU.mult, ALU.add)
+        table_preload = held([P, 1], F32, "table_preload")
+        nc.scalar.activation(out=table_preload[:], in_=one[:], func=ACT.Sqrt)
 
         def copy_on(engine, dst, src):
             if engine == "V":

@@ -18,11 +18,14 @@ ALU = mybir.AluOpType
 
 P = 128
 PACK = 4
-LIST_COLS = S // 16
-PARTS = [2,2,2,4]
 LAST = PACK - 1
-PIECES = PARTS[LAST]
+GROUP = 16
+LIST_COLS = S // GROUP
+LINE = 4
+HALVES, PIECES = 2, 4
 PIECE = S // PIECES
+SUM_BANKS, POWER_BANKS = 5, 3
+LAG = 2
 
 
 def tile_picked_ybutfly_mag_p_kernel(
@@ -32,8 +35,8 @@ def tile_picked_ybutfly_mag_p_kernel(
     with ExitStack() as ctx:
         keep = ctx.enter_context(tc.tile_pool(name="keep", bufs=1))
         work = ctx.enter_context(tc.tile_pool(name="work", bufs=2))
-        sums_ps = ctx.enter_context(tc.psum_pool(name="sums_ps", bufs=5))
-        power_ps = ctx.enter_context(tc.psum_pool(name="power_ps", bufs=3))
+        sums_ps = ctx.enter_context(tc.psum_pool(name="sums_ps", bufs=SUM_BANKS))
+        power_ps = ctx.enter_context(tc.psum_pool(name="power_ps", bufs=POWER_BANKS))
 
         def held(shape, dtype, name):
             return keep.tile(shape, dtype, name=name, align_bytes=64)
@@ -52,6 +55,7 @@ def tile_picked_ybutfly_mag_p_kernel(
 
         nc.vector.memset(scale_table[:, : T // 2].bitcast(I32), 0)
         nc.gpsimd.memset(scale_table[:, T // 2 :].bitcast(I32), 0)
+
         nc.sync.dma_start(out=w1_raw[:], in_=w1.rearrange("(p j) c -> p j c", j=PACK))
         nc.sync.dma_start(offs_sb[:], offs)
         nc.sync.dma_start(b1_sb[:], b1)
@@ -84,78 +88,88 @@ def tile_picked_ybutfly_mag_p_kernel(
         table_preload = held([P, 1], F32, "table_preload")
         nc.scalar.activation(out=table_preload[:], in_=one[:], func=ACT.Sqrt)
 
-        def copy_on(engine, dst, src):
-            if engine == "V":
-                nc.vector.tensor_copy(out=dst, in_=src)
-            else:
-                nc.scalar.copy(out=dst, in_=src)
-
-        def quantise_pair(raw, pair, engine, name):
+        def quantise_pair(raw, pair, copy, name):
             grouped = held([P, 2 * P * PACK], BF16, name + "_bf")
             codes = held([P, 2 * P], U32, name + "_codes")
             scales = held([P, 2 * P], U8, name + "_scales")
-            copy_on(
-                engine,
-                grouped[:].rearrange("p (t m j) -> p m j t", t=2, j=PACK),
-                raw[:].rearrange("p j (m t) -> p m j t", t=PACK)[:, :, :, 2 * pair : 2 * pair + 2],
+            copy(
+                out=grouped[:].rearrange("p (t m j) -> p m j t", t=2, j=PACK),
+                in_=raw[:].rearrange("p j (m t) -> p m j t", t=PACK)[:, :, :, 2 * pair : 2 * pair + 2],
             )
             nc.vector.quantize_mx(out=codes[:].bitcast(FP8X4), scales=scales[:], in_=grouped[:])
             return codes, scales
 
-        w1_q = [quantise_pair(w1_raw, 0, "V", "w1a"), quantise_pair(w1_raw, 1, "S", "w1b")]
+        w1_q = [quantise_pair(w1_raw, 0, nc.vector.tensor_copy, "w1a"), quantise_pair(w1_raw, 1, nc.scalar.copy, "w1b")]
 
         x_scale = held([P, S], U8, "x_scale")
         x_code = held([P, S], U32, "x_code")
         nc.vector.tensor_copy(out=x_scale[:], in_=scale_table[:].indirect(offs_sb[:]))
-        nc.vector.tensor_copy(out=x_code[:], in_=word_table[:].indirect(offs_sb[:]))
+        for h in range(HALVES):
+            nc.vector.tensor_copy(
+                out=x_code[:, h * S // HALVES : (h + 1) * S // HALVES],
+                in_=word_table[:].indirect(offs_sb[:, h * LIST_COLS // HALVES : (h + 1) * LIST_COLS // HALVES]),
+            )
 
-        def product(w_q, t, part):
+        def product(w_q, t, part, steps=1):
             codes, scales = w_q[t // 2]
             cols = slice((t % 2) * P, (t % 2 + 1) * P)
-            acc = sums_ps.tile([P, S], F32, tag="sums", name="acc")
-            nc.tensor.matmul_mx(
-                out=acc[:],
-                lhsT=codes[:, cols].bitcast(FP8X4),
-                lhsT_scale=scales[:, cols],
-                rhs=x_code[:].bitcast(FP8X4),
-                rhs_scale=x_scale[:],
-                start=True,
-                stop=True,
-            )
-            nc.scalar.copy(out=rows[t][:, part], in_=acc[:])
+            width = S // steps
+            for h in range(steps):
+                picked = slice(h * width, (h + 1) * width)
+                acc = sums_ps.tile([P, width], F32, tag="sums", name="acc")
+                nc.tensor.matmul_mx(
+                    out=acc[:],
+                    lhsT=codes[:, cols].bitcast(FP8X4),
+                    lhsT_scale=scales[:, cols],
+                    rhs=x_code[:, picked].bitcast(FP8X4),
+                    rhs_scale=x_scale[:, picked],
+                    start=True,
+                    stop=True,
+                )
+                nc.scalar.copy(out=rows[t][:, part.start + h * width : part.start + (h + 1) * width], in_=acc[:])
 
-        def gather(engine, dst, window, places, scale=None):
-            picked = window.indirect(places)
-            if scale is not None:
-                nc.scalar.activation(out=dst, in_=picked, func=ACT.Copy, scale=scale)
-            elif engine == "V":
-                nc.vector.tensor_copy(out=dst, in_=picked)
+        def gather(on_vector, dst, window, places):
+            if on_vector:
+                nc.vector.tensor_copy(out=dst, in_=window.indirect(places))
             else:
-                nc.scalar.activation(out=dst, in_=picked, func=ACT.Copy)
+                nc.scalar.activation(out=dst, in_=window.indirect(places), func=ACT.Copy)
 
-        PR, PI, XQ, EO = "SVVS", "SSSS", "VSSV", "SSSS"
         pr = [held([P, S], F32, "pr%d" % t) for t in range(PACK)]
         pi = [held([P, S], F32, "pi%d" % t) for t in range(PACK)]
         xr = [held([P, S], F32, "xr%d" % t) for t in range(PACK)]
         xi = [held([P, S], F32, "xi%d" % t) for t in range(PACK)]
-        xp = [held([P, S], F32, "xp%d" % t) for t in range(PACK)]
+        neg_xp = [held([P, S], F32, "xp%d" % t) for t in range(PACK)]
         xq = [held([P, S], F32, "xq%d" % t) for t in range(PACK)]
         mag = held([P, PACK, S], F32, "mag")
         squares = {}
         hid = [held([P, PIECE * PACK], BF16, "hid%d" % h) for h in range(PIECES)]
 
-        def real_partner(t):
-            gather(PR[t], pr[t][:], rows[t][:, 0 : 2 * S], b1_sb[:])
+        def vector_takes_xq(t):
+            return t in (0, LAST)
 
-        def imag_partner(t):
-            gather(PI[t], pi[t][:], rows[t][:, 2 * S : 4 * S], b1_sb[:])
+        def parts_of(t):
+            return PIECES if t == LAST else HALVES
 
-        def first_stage(t):
-            twiddles = rows[t][:].rearrange("p (a b s) -> p a b s", a=2, b=2)[:, :, 1, :]
+        def first_partners(t):
+            gather(not vector_takes_xq(t), pr[t][:], rows[t][:, 0 : 2 * S], b1_sb[:])
+            gather(False, pi[t][:], rows[t][:, 2 * S : 4 * S], b1_sb[:])
+
+        def first_butterfly(t):
             by_pr = work.tile([P, 2, S], F32, tag="by_pr", name="by_pr")
             by_pi = work.tile([P, 2, S], F32, tag="by_pi", name="by_pi")
             u = work.tile([P, S], F32, tag="u", name="u")
             v = work.tile([P, S], F32, tag="v", name="v")
+            if t == LAST:
+                nc.vector.tensor_tensor(by_pr[:, 0, :], rows[t][:, TWR], pr[t][:], ALU.mult)
+                nc.vector.tensor_tensor(by_pi[:, 1, :], rows[t][:, TWI], pi[t][:], ALU.mult)
+                nc.vector.tensor_tensor(u[:], rows[t][:, RE], by_pr[:, 0, :], ALU.add)
+                nc.vector.tensor_tensor(by_pr[:, 1, :], rows[t][:, TWI], pr[t][:], ALU.mult)
+                nc.vector.tensor_tensor(xr[t][:], u[:], by_pi[:, 1, :], ALU.subtract)
+                nc.vector.tensor_tensor(by_pi[:, 0, :], rows[t][:, TWR], pi[t][:], ALU.mult)
+                nc.vector.tensor_tensor(v[:], rows[t][:, IM], by_pr[:, 1, :], ALU.add)
+                nc.vector.tensor_tensor(xi[t][:], v[:], by_pi[:, 0, :], ALU.add)
+                return
+            twiddles = rows[t][:].rearrange("p (a b s) -> p a b s", a=2, b=2)[:, :, 1, :]
             nc.vector.tensor_tensor(by_pr[:], twiddles, pr[t][:].unsqueeze(1).to_broadcast([P, 2, S]), ALU.mult)
             nc.vector.tensor_tensor(by_pi[:], twiddles, pi[t][:].unsqueeze(1).to_broadcast([P, 2, S]), ALU.mult)
             nc.vector.tensor_tensor(u[:], rows[t][:, RE], by_pr[:, 0, :], ALU.add)
@@ -164,93 +178,83 @@ def tile_picked_ybutfly_mag_p_kernel(
             nc.vector.tensor_tensor(xi[t][:], v[:], by_pi[:, 0, :], ALU.add)
 
         def turned_sum(acc, terms):
-            for n, (blk, source) in enumerate(terms):
+            for n, (block, source) in enumerate(terms):
                 nc.tensor.matmul(
-                    acc[:, blk * P : (blk + 1) * P], lhsT=source, rhs=ident[:], is_transpose=True,
+                    acc[:, block * P : (block + 1) * P], lhsT=source, rhs=ident[:], is_transpose=True,
                     start=(n == 0), stop=(n == len(terms) - 1),
                 )
 
         def second_partners(t):
-            width = S // PARTS[t]
-            for h in range(PARTS[t]):
+            width = S // parts_of(t)
+            for h in range(parts_of(t)):
                 cols = slice(h * width, (h + 1) * width)
-                places = b2_sb[:, h * width // 16 : (h + 1) * width // 16]
-                gather("S", xp[t][:, cols], xr[t][:], places, scale=-1.0)
-                gather(XQ[t], xq[t][:, cols], xi[t][:], places)
+                places = b2_sb[:, h * width // GROUP : (h + 1) * width // GROUP]
+                nc.scalar.activation(out=neg_xp[t][:, cols], in_=xr[t][:].indirect(places), func=ACT.Copy, scale=-1.0)
+                gather(vector_takes_xq(t), xq[t][:, cols], xi[t][:], places)
 
         def square_parts(t):
-            width = S // PARTS[t]
-            nblk = width // P
-            for h in range(PARTS[t]):
+            width = S // parts_of(t)
+            blocks = width // P
+            for h in range(parts_of(t)):
                 y = sums_ps.tile([P, 2 * width], F32, tag="sums", name="y")
-                sources = [(0, xr[t]), (nblk, xi[t]), (0, xp[t]), (nblk, xq[t])]
-                if t == LAST:
-                    sources = [(0, xr[t]), (nblk, xi[t]), (nblk, xq[t]), (0, xp[t])]
+                gathered = [(0, neg_xp[t]), (blocks, xq[t])]
+                sources = [(0, xr[t]), (blocks, xi[t])] + (gathered[::-1] if t == LAST else gathered)
                 terms = []
                 for first, source in sources:
-                    for k in range(nblk):
+                    for k in range(blocks):
                         terms.append((first + k, source[:, h * width + k * P : h * width + (k + 1) * P]))
                 turned_sum(y, terms)
                 squares[t, h] = held([P, 2 * width], F32, "sq%d_%d" % (t, h))
                 nc.scalar.activation(out=squares[t, h][:], in_=y[:], func=ACT.Square)
 
         def magnitudes(t):
-            width = S // PARTS[t]
-            nblk = width // P
-            for h in range(PARTS[t]):
+            width = S // parts_of(t)
+            blocks = width // P
+            for h in range(parts_of(t)):
                 power = power_ps.tile([P, width], F32, tag="power", name="power")
-                turned_sum(power, [(k % nblk, squares[t, h][:, k * P : (k + 1) * P]) for k in range(2 * nblk)])
+                turned_sum(power, [(k % blocks, squares[t, h][:, k * P : (k + 1) * P]) for k in range(2 * blocks)])
                 nc.scalar.activation(out=mag[:, t, h * width : (h + 1) * width], in_=power[:], func=ACT.Sqrt, bias=eps[:])
 
-        product(w1_q, 0, RE)
-        w2_q = [quantise_pair(w2_raw, 0, "V", "w2a")]
+        product(w1_q, 0, RE, steps=HALVES)
+        w2_q = [quantise_pair(w2_raw, 0, nc.vector.tensor_copy, "w2a")]
         product(w2_q, 0, IM)
-        real_partner(0)
-        imag_partner(0)
-        w2_q.append(quantise_pair(w2_raw, 1, "V", "w2b"))
-        product(w1_q, 1, RE)
-        product(w2_q, 1, IM)
-        real_partner(1)
-        imag_partner(1)
-        first_stage(0)
-        product(w1_q, 2, RE)
-        product(w2_q, 2, IM)
-        real_partner(2)
-        imag_partner(2)
-        first_stage(1)
-        second_partners(0)
-        product(w1_q, 3, RE)
-        product(w2_q, 3, IM)
-        square_parts(0)
-        real_partner(3)
-        imag_partner(3)
-        magnitudes(0)
-        first_stage(2)
-        second_partners(1)
-        square_parts(1)
-        magnitudes(1)
-        first_stage(3)
-        second_partners(2)
-        second_partners(3)
-        square_parts(2)
-        magnitudes(2)
-        square_parts(3)
-        magnitudes(3)
+        first_partners(0)
+        w2_q.append(quantise_pair(w2_raw, 1, nc.vector.tensor_copy, "w2b"))
+
+        for t in range(PACK):
+            ahead, behind = t + 1, t - LAG
+            if behind >= 0:
+                second_partners(behind)
+            if ahead < PACK:
+                product(w1_q, ahead, RE)
+                product(w2_q, ahead, IM)
+            if behind >= 0:
+                square_parts(behind)
+            if ahead < PACK:
+                first_partners(ahead)
+            if behind >= 0:
+                magnitudes(behind)
+            first_butterfly(t)
+        for t in range(PACK - LAG, PACK):
+            second_partners(t)
+        for t in range(PACK - LAG, PACK):
+            square_parts(t)
+            magnitudes(t)
 
         w3_bf = held([P, N * PACK], BF16, "w3_bf")
         w3_codes = held([P, N], U32, "w3_codes")
         w3_scales = held([P, N], U8, "w3_scales")
         nc.vector.tensor_copy(
-            out=w3_bf[:].rearrange("p (c i j) -> p c j i", i=4, j=PACK),
-            in_=w3_raw[:].rearrange("p j (c i) -> p c j i", i=4),
+            out=w3_bf[:].rearrange("p (c i j) -> p c j i", i=LINE, j=PACK),
+            in_=w3_raw[:].rearrange("p j (c i) -> p c j i", i=LINE),
         )
         nc.vector.quantize_mx(out=w3_codes[:].bitcast(FP8X4), scales=w3_scales[:], in_=w3_bf[:])
 
         for h in range(PIECES):
             nc.vector.tensor_tensor(
-                hid[h][:].rearrange("p (c i t) -> p c t i", i=4, t=PACK)[:, :, 0:LAST, :],
-                mag[:, 0:LAST, h * PIECE : (h + 1) * PIECE].rearrange("p t (c i) -> p c t i", i=4),
-                unit_sb[:, 0:LAST].unsqueeze(1).unsqueeze(3).to_broadcast([P, PIECE // 4, LAST, 4]),
+                hid[h][:].rearrange("p (c i t) -> p c t i", i=LINE, t=PACK)[:, :, 0:LAST, :],
+                mag[:, 0:LAST, h * PIECE : (h + 1) * PIECE].rearrange("p t (c i) -> p c t i", i=LINE),
+                unit_sb[:, 0:LAST].unsqueeze(1).unsqueeze(3).to_broadcast([P, PIECE // LINE, LAST, LINE]),
                 ALU.mult,
             )
 
@@ -263,11 +267,11 @@ def tile_picked_ybutfly_mag_p_kernel(
             hid_codes = held([P, PIECE], U32, "hid_codes%d" % h)
             hid_scales = held([P, PIECE], U8, "hid_scales%d" % h)
             nc.vector.quantize_mx(out=hid_codes[:].bitcast(FP8X4), scales=hid_scales[:], in_=hid[h][:])
-            acc = sums_ps.tile([P, 2 * PIECE], F32, tag="sums", name="acc_out")
-            for m in range(2):
+            acc_out = sums_ps.tile([P, (N // P) * PIECE], F32, tag="sums", name="acc_out")
+            for m in range(N // P):
                 cols = slice(m * P, (m + 1) * P)
                 nc.tensor.matmul_mx(
-                    out=acc[:, m * PIECE : (m + 1) * PIECE],
+                    out=acc_out[:, m * PIECE : (m + 1) * PIECE],
                     lhsT=w3_codes[:, cols].bitcast(FP8X4),
                     lhsT_scale=w3_scales[:, cols],
                     rhs=hid_codes[:].bitcast(FP8X4),
@@ -275,8 +279,8 @@ def tile_picked_ybutfly_mag_p_kernel(
                     start=True,
                     stop=True,
                 )
-            result = held([P, 2, PIECE], F32, "result%d" % h)
-            copy_on(EO[h], result[:].rearrange("p m n -> p (m n)"), acc[:])
+            result = held([P, N // P, PIECE], F32, "result%d" % h)
+            nc.scalar.copy(out=result[:].rearrange("p m n -> p (m n)"), in_=acc_out[:])
             nc.sync.dma_start(
                 out=out.rearrange("(m p) s -> p m s", p=P)[:, :, h * PIECE : (h + 1) * PIECE], in_=result[:]
             )

from contextlib import ExitStack

import concourse.mybir as mybir
from concourse.masks import make_identity

K, T, S, N, H = 512, 2048, 512, 256, 512
FLOPS = 2 * K * H * S * 2 + 2 * H * N * S

F32 = mybir.dt.float32
BF16 = mybir.dt.bfloat16
I32 = mybir.dt.int32
U32 = mybir.dt.uint32
U16 = mybir.dt.uint16
U8 = mybir.dt.uint8
FP8X4 = mybir.dt.float8_e4m3fn_x4
ACT = mybir.ActivationFunctionType
ALU = mybir.AluOpType

P = 128
PACK = 4
LAST = PACK - 1
GROUP = 16
LIST_COLS = S // GROUP
LINE = 4
HALVES, PIECES = 2, 4
PIECE = S // PIECES
SUM_BANKS, POWER_BANKS = 5, 3
LAG = 2


def tile_picked_ybutfly_mag_p_kernel(
    tc, x_words, x_scales, w1, w2, twr, twi, unit, w3, offs, b1, b2, out
):
    nc = tc.nc
    with ExitStack() as ctx:
        keep = ctx.enter_context(tc.tile_pool(name="keep", bufs=1))
        work = ctx.enter_context(tc.tile_pool(name="work", bufs=2))
        sums_ps = ctx.enter_context(tc.psum_pool(name="sums_ps", bufs=SUM_BANKS))
        power_ps = ctx.enter_context(tc.psum_pool(name="power_ps", bufs=POWER_BANKS))

        def held(shape, dtype, name):
            return keep.tile(shape, dtype, name=name, align_bytes=64)

        offs_sb = held([P, LIST_COLS], U16, "offs_sb")
        b1_sb = held([P, LIST_COLS], U16, "b1_sb")
        b2_sb = held([P, LIST_COLS], U16, "b2_sb")
        scale_table = held([P, T], U8, "scale_table")
        word_table = held([P, T], U32, "word_table")
        w1_raw = held([P, PACK, H], F32, "w1_raw")
        w2_raw = held([P, PACK, H], F32, "w2_raw")
        w3_raw = held([P, PACK, N], F32, "w3_raw")
        unit_sb = held([P, PACK], F32, "unit_sb")
        rows = [held([P, 4 * S], F32, "rows%d" % t) for t in range(PACK)]
        RE, TWR, IM, TWI = [slice(n * S, (n + 1) * S) for n in range(4)]

        nc.vector.memset(scale_table[:, : T // 2].bitcast(I32), 0)
        nc.gpsimd.memset(scale_table[:, T // 2 :].bitcast(I32), 0)

        nc.sync.dma_start(out=w1_raw[:], in_=w1.rearrange("(p j) c -> p j c", j=PACK))
        nc.sync.dma_start(offs_sb[:], offs)
        nc.sync.dma_start(b1_sb[:], b1)
        for q in range(4):
            nc.sync.dma_start(
                out=scale_table[32 * q : 32 * q + 4, :].bitcast(I32),
                in_=x_scales[0, 4 * q : 4 * q + 4, :].bitcast(I32),
            )
        nc.sync.dma_start(
            out=word_table[:].bitcast(I32),
            in_=x_words[0].rearrange("p n t -> p (n t)").bitcast(I32),
        )
        nc.sync.dma_start(out=w2_raw[:], in_=w2.rearrange("(p j) c -> p j c", j=PACK))
        twr_rows = twr.rearrange("(p t) s -> p t s", t=PACK)
        twi_rows = twi.rearrange("(p t) s -> p t s", t=PACK)
        for t in range(PACK):
            nc.sync.dma_start(out=rows[t][:, TWR], in_=twr_rows[:, t, :])
            nc.sync.dma_start(out=rows[t][:, TWI], in_=twi_rows[:, t, :])
            if t == 0:
                nc.sync.dma_start(b2_sb[:], b2)
        nc.sync.dma_start(out=unit_sb[:], in_=unit.rearrange("(p t) o -> p (t o)", t=PACK))
        nc.sync.dma_start(out=w3_raw[:], in_=w3.rearrange("(p j) c -> p j c", j=PACK))

        ident = held([P, P], F32, "ident")
        make_identity(nc, ident[:])
        one = held([P, 1], F32, "one")
        eps = held([P, 1], F32, "eps")
        nc.gpsimd.memset(one[:], 1.0)
        nc.gpsimd.tensor_scalar(eps[:], one[:], 0.1, 0.0, ALU.mult, ALU.add)
        table_preload = held([P, 1], F32, "table_preload")
        nc.scalar.activation(out=table_preload[:], in_=one[:], func=ACT.Sqrt)

        def quantise_pair(raw, pair, copy, name):
            grouped = held([P, 2 * P * PACK], BF16, name + "_bf")
            codes = held([P, 2 * P], U32, name + "_codes")
            scales = held([P, 2 * P], U8, name + "_scales")
            copy(
                out=grouped[:].rearrange("p (t m j) -> p m j t", t=2, j=PACK),
                in_=raw[:].rearrange("p j (m t) -> p m j t", t=PACK)[:, :, :, 2 * pair : 2 * pair + 2],
            )
            nc.vector.quantize_mx(out=codes[:].bitcast(FP8X4), scales=scales[:], in_=grouped[:])
            return codes, scales

        w1_q = [quantise_pair(w1_raw, 0, nc.vector.tensor_copy, "w1a"), quantise_pair(w1_raw, 1, nc.scalar.copy, "w1b")]

        x_scale = held([P, S], U8, "x_scale")
        x_code = held([P, S], U32, "x_code")
        nc.vector.tensor_copy(out=x_scale[:], in_=scale_table[:].indirect(offs_sb[:]))
        for h in range(HALVES):
            nc.vector.tensor_copy(
                out=x_code[:, h * S // HALVES : (h + 1) * S // HALVES],
                in_=word_table[:].indirect(offs_sb[:, h * LIST_COLS // HALVES : (h + 1) * LIST_COLS // HALVES]),
            )

        def product(w_q, t, part, steps=1):
            codes, scales = w_q[t // 2]
            cols = slice((t % 2) * P, (t % 2 + 1) * P)
            width = S // steps
            for h in range(steps):
                picked = slice(h * width, (h + 1) * width)
                acc = sums_ps.tile([P, width], F32, tag="sums", name="acc")
                nc.tensor.matmul_mx(
                    out=acc[:],
                    lhsT=codes[:, cols].bitcast(FP8X4),
                    lhsT_scale=scales[:, cols],
                    rhs=x_code[:, picked].bitcast(FP8X4),
                    rhs_scale=x_scale[:, picked],
                    start=True,
                    stop=True,
                )
                nc.scalar.copy(out=rows[t][:, part.start + h * width : part.start + (h + 1) * width], in_=acc[:])

        def gather(on_vector, dst, window, places):
            if on_vector:
                nc.vector.tensor_copy(out=dst, in_=window.indirect(places))
            else:
                nc.scalar.activation(out=dst, in_=window.indirect(places), func=ACT.Copy)

        pr = [held([P, S], F32, "pr%d" % t) for t in range(PACK)]
        pi = [held([P, S], F32, "pi%d" % t) for t in range(PACK)]
        xr = [held([P, S], F32, "xr%d" % t) for t in range(PACK)]
        xi = [held([P, S], F32, "xi%d" % t) for t in range(PACK)]
        neg_xp = [held([P, S], F32, "xp%d" % t) for t in range(PACK)]
        xq = [held([P, S], F32, "xq%d" % t) for t in range(PACK)]
        mag = held([P, PACK, S], F32, "mag")
        squares = {}
        hid = [held([P, PIECE * PACK], BF16, "hid%d" % h) for h in range(PIECES)]

        def vector_takes_xq(t):
            return t in (0, LAST)

        def parts_of(t):
            return PIECES if t == LAST else HALVES

        def first_partners(t):
            gather(not vector_takes_xq(t), pr[t][:], rows[t][:, 0 : 2 * S], b1_sb[:])
            gather(False, pi[t][:], rows[t][:, 2 * S : 4 * S], b1_sb[:])

        def first_butterfly(t):
            by_pr = work.tile([P, 2, S], F32, tag="by_pr", name="by_pr")
            by_pi = work.tile([P, 2, S], F32, tag="by_pi", name="by_pi")
            u = work.tile([P, S], F32, tag="u", name="u")
            v = work.tile([P, S], F32, tag="v", name="v")
            if t == LAST:
                nc.vector.tensor_tensor(by_pr[:, 0, :], rows[t][:, TWR], pr[t][:], ALU.mult)
                nc.vector.tensor_tensor(by_pi[:, 1, :], rows[t][:, TWI], pi[t][:], ALU.mult)
                nc.vector.tensor_tensor(u[:], rows[t][:, RE], by_pr[:, 0, :], ALU.add)
                nc.vector.tensor_tensor(by_pr[:, 1, :], rows[t][:, TWI], pr[t][:], ALU.mult)
                nc.vector.tensor_tensor(xr[t][:], u[:], by_pi[:, 1, :], ALU.subtract)
                nc.vector.tensor_tensor(by_pi[:, 0, :], rows[t][:, TWR], pi[t][:], ALU.mult)
                nc.vector.tensor_tensor(v[:], rows[t][:, IM], by_pr[:, 1, :], ALU.add)
                nc.vector.tensor_tensor(xi[t][:], v[:], by_pi[:, 0, :], ALU.add)
                return
            twiddles = rows[t][:].rearrange("p (a b s) -> p a b s", a=2, b=2)[:, :, 1, :]
            nc.vector.tensor_tensor(by_pr[:], twiddles, pr[t][:].unsqueeze(1).to_broadcast([P, 2, S]), ALU.mult)
            nc.vector.tensor_tensor(by_pi[:], twiddles, pi[t][:].unsqueeze(1).to_broadcast([P, 2, S]), ALU.mult)
            nc.vector.tensor_tensor(u[:], rows[t][:, RE], by_pr[:, 0, :], ALU.add)
            nc.vector.tensor_tensor(v[:], rows[t][:, IM], by_pr[:, 1, :], ALU.add)
            nc.vector.tensor_tensor(xr[t][:], u[:], by_pi[:, 1, :], ALU.subtract)
            nc.vector.tensor_tensor(xi[t][:], v[:], by_pi[:, 0, :], ALU.add)

        def turned_sum(acc, terms):
            for n, (block, source) in enumerate(terms):
                nc.tensor.matmul(
                    acc[:, block * P : (block + 1) * P], lhsT=source, rhs=ident[:], is_transpose=True,
                    start=(n == 0), stop=(n == len(terms) - 1),
                )

        def second_partners(t):
            width = S // parts_of(t)
            for h in range(parts_of(t)):
                cols = slice(h * width, (h + 1) * width)
                places = b2_sb[:, h * width // GROUP : (h + 1) * width // GROUP]
                nc.scalar.activation(out=neg_xp[t][:, cols], in_=xr[t][:].indirect(places), func=ACT.Copy, scale=-1.0)
                gather(vector_takes_xq(t), xq[t][:, cols], xi[t][:], places)

        def square_parts(t):
            width = S // parts_of(t)
            blocks = width // P
            for h in range(parts_of(t)):
                y = sums_ps.tile([P, 2 * width], F32, tag="sums", name="y")
                gathered = [(0, neg_xp[t]), (blocks, xq[t])]
                sources = [(0, xr[t]), (blocks, xi[t])] + (gathered[::-1] if t == LAST else gathered)
                terms = []
                for first, source in sources:
                    for k in range(blocks):
                        terms.append((first + k, source[:, h * width + k * P : h * width + (k + 1) * P]))
                turned_sum(y, terms)
                squares[t, h] = held([P, 2 * width], F32, "sq%d_%d" % (t, h))
                nc.scalar.activation(out=squares[t, h][:], in_=y[:], func=ACT.Square)

        def magnitudes(t):
            width = S // parts_of(t)
            blocks = width // P
            for h in range(parts_of(t)):
                power = power_ps.tile([P, width], F32, tag="power", name="power")
                turned_sum(power, [(k % blocks, squares[t, h][:, k * P : (k + 1) * P]) for k in range(2 * blocks)])
                nc.scalar.activation(out=mag[:, t, h * width : (h + 1) * width], in_=power[:], func=ACT.Sqrt, bias=eps[:])

        product(w1_q, 0, RE, steps=HALVES)
        w2_q = [quantise_pair(w2_raw, 0, nc.vector.tensor_copy, "w2a")]
        product(w2_q, 0, IM)
        first_partners(0)
        w2_q.append(quantise_pair(w2_raw, 1, nc.vector.tensor_copy, "w2b"))

        for t in range(PACK):
            ahead, behind = t + 1, t - LAG
            if behind >= 0:
                second_partners(behind)
            if ahead < PACK:
                product(w1_q, ahead, RE)
                product(w2_q, ahead, IM)
            if behind >= 0:
                square_parts(behind)
            if ahead < PACK:
                first_partners(ahead)
            if behind >= 0:
                magnitudes(behind)
            first_butterfly(t)
        for t in range(PACK - LAG, PACK):
            second_partners(t)
        for t in range(PACK - LAG, PACK):
            square_parts(t)
            magnitudes(t)

        w3_bf = held([P, N * PACK], BF16, "w3_bf")
        w3_codes = held([P, N], U32, "w3_codes")
        w3_scales = held([P, N], U8, "w3_scales")
        nc.vector.tensor_copy(
            out=w3_bf[:].rearrange("p (c i j) -> p c j i", i=LINE, j=PACK),
            in_=w3_raw[:].rearrange("p j (c i) -> p c j i", i=LINE),
        )
        nc.vector.quantize_mx(out=w3_codes[:].bitcast(FP8X4), scales=w3_scales[:], in_=w3_bf[:])

        for h in range(PIECES):
            nc.vector.tensor_tensor(
                hid[h][:].rearrange("p (c i t) -> p c t i", i=LINE, t=PACK)[:, :, 0:LAST, :],
                mag[:, 0:LAST, h * PIECE : (h + 1) * PIECE].rearrange("p t (c i) -> p c t i", i=LINE),
                unit_sb[:, 0:LAST].unsqueeze(1).unsqueeze(3).to_broadcast([P, PIECE // LINE, LAST, LINE]),
                ALU.mult,
            )

        for h in range(PIECES):
            nc.vector.tensor_scalar(
                hid[h][:].rearrange("p (n t) -> p n t", t=PACK)[:, :, LAST],
                mag[:, LAST, h * PIECE : (h + 1) * PIECE],
                unit_sb[:, LAST : LAST + 1], None, ALU.mult,
            )
            hid_codes = held([P, PIECE], U32, "hid_codes%d" % h)
            hid_scales = held([P, PIECE], U8, "hid_scales%d" % h)
            nc.vector.quantize_mx(out=hid_codes[:].bitcast(FP8X4), scales=hid_scales[:], in_=hid[h][:])
            acc_out = sums_ps.tile([P, (N // P) * PIECE], F32, tag="sums", name="acc_out")
            for m in range(N // P):
                cols = slice(m * P, (m + 1) * P)
                nc.tensor.matmul_mx(
                    out=acc_out[:, m * PIECE : (m + 1) * PIECE],
                    lhsT=w3_codes[:, cols].bitcast(FP8X4),
                    lhsT_scale=w3_scales[:, cols],
                    rhs=hid_codes[:].bitcast(FP8X4),
                    rhs_scale=hid_scales[:],
                    start=True,
                    stop=True,
                )
            result = held([P, N // P, PIECE], F32, "result%d" % h)
            nc.scalar.copy(out=result[:].rearrange("p m n -> p (m n)"), in_=acc_out[:])
            nc.sync.dma_start(
                out=out.rearrange("(m p) s -> p m s", p=P)[:, :, h * PIECE : (h + 1) * PIECE], in_=result[:]
            )
